import numpy as np, ml_dtypes
CORES = [30,158,46,174,86,214]
N = 6
TK = 128
def setup_inputs(rng):
    return {"x": rng.standard_normal((N, 128, TK), dtype=np.float32).astype(ml_dtypes.bfloat16), "w": rng.standard_normal((N, 128, 128), dtype=np.float32).astype(ml_dtypes.bfloat16)}
def setup_inputs_big(rng):
    d = setup_inputs(rng)
    for k in ("x", "w"): d[k] = (d[k].astype(np.float32) * 1024.0).astype(d[k].dtype)
    return d
def setup_inputs_small(rng):
    d = setup_inputs(rng)
    for k in ("x", "w"): d[k] = (d[k].astype(np.float32) * (1 / 1024.0)).astype(d[k].dtype)
    return d
def setup_inputs_apart(rng):
    d = setup_inputs(rng)
    f = (10.0 ** rng.permutation(np.linspace(-1.5, 1.5, N))).astype(np.float32).reshape(N, 1, 1)
    for k in ("x", "w"): d[k] = (d[k].astype(np.float32) * f).astype(d[k].dtype)
    return d
def setup_inputs_neg(rng):
    d = setup_inputs(rng)
    d["x"] = (np.abs(d["x"].astype(np.float32)) * 1048576.0).astype(d["x"].dtype); d["w"] = (-np.abs(d["w"].astype(np.float32))).astype(d["w"].dtype)
    return d
def reference(x, w):
    X, W = x.astype(np.float64), w.astype(np.float64)
    y = np.stack([np.max([W[j].T @ X[r] for j in range(N)], axis=0) for r in range(N)])
    return {"y": y.astype(ml_dtypes.bfloat16)}

from concourse.bass import DstId, RemoteDMATransfer
from concourse.mybir import AluOpType

N = 6
D = 128

SCRATCH = {
    "wall": ("sbuf", [128, N * D], "bfloat16"),
    "xs": ("sbuf", [128, D], "bfloat16"),
    "acc0": ("sbuf", [128, D], "float32"),
    "acc1": ("sbuf", [128, D], "float32"),
    "ys": ("sbuf", [128, D], "bfloat16"),
}
for _j in range(N):
    SCRATCH["p%d" % _j] = ("psum", [128, 512], "float32")

SEMAPHORES = ["wl", "xl", "sent", "vs", "st"] + ["arr%d" % j for j in range(N)] + ["mm%d" % j for j in range(N)]


def _partners(rank, T, topo):
    n = len(T.cores)
    rounds = []
    for q in range(n - 1):
        pairs = [(n - 1, q)] + [((q + k) % (n - 1), (q - k) % (n - 1)) for k in range(1, n // 2)]
        rounds.append(pairs)
    rounds.sort(key=lambda ps: sum(0 if topo.same_plane(T.cores[a], T.cores[b]) else 1 for a, b in ps), reverse=True)
    out = []
    for pairs in rounds:
        for a, b in pairs:
            if a == rank:
                out.append(b)
            elif b == rank:
                out.append(a)
    return out


def _count(mask):
    return sum((mask >> b) & 1 for b in range(16))


def rank_program(g, core, T, topo):
    rank = T.rank_of(core)
    if rank is None:
        return
    S = T.sem

    def slot(j):
        return T.wall[:, j * D:(j + 1) * D]

    peers = _partners(rank, T, topo)

    g.sync.dma_start(slot(rank), T.w[:]).then_inc(S.wl, 16)
    g.sync.dma_start(T.xs[:], T.x[:]).then_inc(S.xl, 16)

    mask = topo.mask(core, T.cores[peers[0]])
    for p in peers:
        mask &= topo.mask(core, T.cores[p])
    ids = []
    for p in peers:
        rid, pid = topo.addr(T.cores[p], core)
        ids.append(DstId(rid=rid, pnc=pid))
    g.wait_ge(S.wl, 16)
    g.remote_dma_fused(
        [RemoteDMATransfer(dst_ids=ids, dma_engine_mask=mask, remote_sem=S["arr%d" % rank],
                           srcs=[slot(rank)], dsts=[slot(rank) for _ in peers], alu_op=0)],
        local_sem=S.sent)

    g.tensor.wait_ge(S.wl, 16)
    g.tensor.wait_ge(S.xl, 16)
    g.tensor.matmul(T["p%d" % rank][:, 0:D], slot(rank), T.xs[:], start=True, stop=True).then_inc(S["mm%d" % rank], 1)
    for p in peers:
        pm = topo.mask(T.cores[p], core)
        for q in T.cores:
            if q != T.cores[p]:
                pm &= topo.mask(T.cores[p], q)
        g.tensor.wait_ge(S["arr%d" % p], _count(pm))
        g.tensor.matmul(T["p%d" % p][:, 0:D], slot(p), T.xs[:], start=True, stop=True).then_inc(S["mm%d" % p], 1)

    acc = [T.acc0, T.acc1]
    g.vector.wait_ge(S["mm%d" % rank], 1)
    g.vector.tensor_copy(acc[0][:], T["p%d" % rank][:, 0:D]).then_inc(S.vs, 1)
    for k, p in enumerate(peers):
        g.vector.wait_ge(S["mm%d" % p], 1)
        g.vector.wait_ge(S.vs, k + 1)
        out = T.ys if k == len(peers) - 1 else acc[(k + 1) % 2]
        g.vector.tensor_tensor(out[:], acc[k % 2][:], T["p%d" % p][:, 0:D], AluOpType.max).then_inc(S.vs, 1)

    g.sync.wait_ge(S.vs, len(peers) + 1)
    g.sync.dma_start(T.y[:], T.ys[:]).then_inc(S.st, 16)
    g.sync.wait_ge(S.st, 16)
    g.wait_ge(S.sent, _count(mask))
